import numpy as np
import ml_dtypes


def mxq(x, axis, fmt="e4m3"):
    dtype, down = {"e4m3": (ml_dtypes.float8_e4m3fn, 7), "e5m2": (ml_dtypes.float8_e5m2, 14)}[fmt]
    v = np.moveaxis(np.asarray(x, np.float32).astype(ml_dtypes.bfloat16).astype(np.float64), axis, -1)
    blocks = v.reshape(v.shape[:-1] + (-1, 32))
    amax = np.abs(blocks).max(-1, keepdims=True)
    byte = np.maximum(np.where(amax > 0, np.frexp(amax)[1] - 1 + 127, 0) - down, 1)
    scale = np.exp2(byte - 127.0)
    codes = (blocks / scale).astype(np.float32).astype(dtype).astype(np.float64)
    return np.moveaxis((codes * scale).reshape(v.shape), -1, axis)


WIDE = False


def mx_kscale(k, group=512):
    if not WIDE:
        return np.ones(k)
    levels = np.array([10, -10, 5, -5, 0])
    if group != 512:
        return np.exp2(np.random.permutation(np.resize(levels, k // group))).repeat(group)
    if k % 512:
        return np.exp2(np.random.permutation(np.resize(levels, k // 32))).repeat(32)
    a = np.empty((k // 512, 16))
    for p in range(k // 512):
        a[p, :8] = np.random.permutation(np.resize(levels, 8))
        for g in range(8):
            far = levels[np.abs(levels - a[p, g]) >= 10]
            a[p, g + 8] = far[np.random.randint(len(far))]
    return np.exp2(a.ravel()).repeat(32)


def f64(x):
    return np.asarray(x).astype(np.float64)


E2M1 = np.array([0.0, 0.5, 1.0, 1.5, 2.0, 3.0, 4.0, 6.0, -0.0, -0.5, -1.0, -1.5, -2.0, -3.0, -4.0, -6.0])


def pack_group(w):
    k, n = w.shape
    w = f64(np.asarray(w, np.float32).astype(ml_dtypes.bfloat16)).reshape(k // 32, 32, n)
    amax = np.abs(w).max(1)
    mant, ex = np.frexp(amax / 6.0)
    byte = np.clip(np.where(amax > 0, np.where(mant > 0.5, ex, ex - 1) + 127, 1), 1, 254)
    scaled = (w * np.exp2(127.0 - byte)[:, None, :]).reshape(k, n).astype(np.float32)
    c = np.ascontiguousarray(scaled.reshape(k // 4, 4, n).transpose(0, 2, 1)).astype(ml_dtypes.float4_e2m1fn).view(np.uint8) & 0xF
    return np.ascontiguousarray((c[..., 0::2] | (c[..., 1::2] << 4)).reshape(k // 4, 2 * n)), byte.astype(np.uint8)


def unpack_group(words, scales):
    p, n = words.shape[0], scales.shape[1]
    words = np.ascontiguousarray(words).reshape(p, n, 2)
    nib = np.empty((p, n, 4), np.uint8)
    nib[..., 0::2] = words & 0xF
    nib[..., 1::2] = words >> 4
    return E2M1[nib].transpose(0, 2, 1).reshape(4 * p, n) * np.repeat(np.exp2(scales.astype(np.float64) - 127.0), 32, axis=0)


G, D, M, N = 4, 256, 128, 1024


def setup_inputs():
    n = np.random.standard_normal
    s = mx_kscale(D, 0)[:, None]
    w_ = [pack_group(w) for w in n((G, D, M)) / np.sqrt(D) / s]
    u_ = [pack_group(w) for w in n((G, D, M)) / np.sqrt(D) / s]
    return {
        "x": (n((G, D, N)) * s).astype(np.float32),
        "w_words": np.stack([w[0] for w in w_]),
        "w_scales": np.stack([w[1] for w in w_]),
        "u_words": np.stack([w[0] for w in u_]),
        "u_scales": np.stack([w[1] for w in u_]),
    }


def reference(x, w_words, w_scales, u_words, u_scales):
    xq = mxq(f64(x), 1, "e4m3")
    h = np.stack([unpack_group(w_words[g], w_scales[g]) for g in range(G)]).transpose(0, 2, 1) @ xq
    g = np.stack([unpack_group(u_words[g], u_scales[g]) for g in range(G)]).transpose(0, 2, 1) @ xq
    y = 1.0 / (1.0 + np.exp(-(h))) * g
    return y

@@ -1,0 +1,213 @@
+from contextlib import ExitStack
+
+import concourse.mybir as mybir
+
+G, D, M, N = 4, 256, 128, 1024
+FLOPS = 2 * 2 * G * D * M * N
+
+F32 = mybir.dt.float32
+BF16 = mybir.dt.bfloat16
+I32 = mybir.dt.int32
+U32 = mybir.dt.uint32
+U8 = mybir.dt.uint8
+FP8X4 = mybir.dt.float8_e4m3fn_x4
+FP4X4 = mybir.dt.float4_e2m1fn_x4
+ACT = mybir.ActivationFunctionType
+ALU = mybir.AluOpType
+
+P = 128
+ROWS = 64
+NT = 512
+LOADS = [[0,256],[256,512],[512,768],[768,1024],[1024,1280],[1280,1536],[1536,1792],[1792,2048]]
+IL = 4
+PLAN = [["memset"],
+    ["words","s",0],
+    ["words","s",1],
+    ["scales","s",0,0],
+    ["scales","s",0,1],
+    ["scales","s",0,2],
+    ["scales","s",0,3],
+    ["load",0],
+    ["load",1],
+    ["warm"],
+    ["scales","s",1,0],
+    ["scales","s",1,1],
+    ["scales","s",1,2],
+    ["scales","s",1,3],
+    ["load",2],
+    ["load",3],
+    ["load",4],
+    ["load",5],
+    ["load",6],
+    ["load",7],
+    ["copy","v",0,256],
+    ["quant",0,256],
+    ["copy","v",256,416],
+    ["copy","s",416,512],
+    ["quant",256,512],
+    ["mm",0,0,0,0],
+    ["mm",1,0,0,1],
+    ["copy","v",512,704],
+    ["copy","s",704,768],
+    ["quant",512,768],
+    ["sig",0,0,0,0,512],
+    ["sig",1,0,0,0,512],
+    ["mul",0,1,0,0,512],
+    ["copy","v",768,928],
+    ["copy","s",928,1024],
+    ["quant",768,1024],
+    ["mm",0,0,512,2],
+    ["mm",1,0,512,3],
+    ["mul",1,1,0,0,512],
+    ["store","y",0,2,0,512],
+    ["copy","v",1024,1152],
+    ["copy","s",1152,1280],
+    ["quant",1024,1280],
+    ["sig",0,2,512,512,1024],
+    ["sig",1,2,512,512,1024],
+    ["mul",0,3,512,512,1024],
+    ["copy","v",1280,1440],
+    ["copy","s",1440,1536],
+    ["quant",1280,1536],
+    ["mm",0,1,1024,0],
+    ["mm",1,1,1024,1],
+    ["mul",1,3,512,512,1024],
+    ["store","y",0,2,512,1024],
+    ["copy","v",1536,1664],
+    ["copy","s",1664,1792],
+    ["quant",1536,1792],
+    ["sig",0,0,1024,1024,1536],
+    ["copy","v",1792,1952],
+    ["copy","s",1952,2048],
+    ["mul",0,1,1024,1024,1536],
+    ["quant",1792,2048],
+    ["mm",0,1,1536,2],
+    ["mm",1,1,1536,3],
+    ["sig",1,0,1024,1024,1536],
+    ["mul",1,1,1024,1024,1536],
+    ["store","y",0,2,1024,1536],
+    ["sig",0,2,1536,1536,2048],
+    ["sig",1,2,1536,1536,1792],
+    ["sig",1,2,1536,1792,2048],
+    ["mul",0,3,1536,1536,2048],
+    ["store","y",0,1,1536,2048],
+    ["mul",1,3,1536,1536,1792],
+    ["store","y",1,2,1536,1792],
+    ["mul",1,3,1536,1792,2048],
+    ["store","y",1,2,1792,2048]]
+
+
+def tile_rows_gglu_sigmoid_kernel(tc, x, w_words, w_scales, u_words, u_scales, out):
+    nc = tc.nc
+    with ExitStack() as ctx:
+        sb = ctx.enter_context(tc.tile_pool(name="sb", bufs=1))
+        ps = ctx.enter_context(tc.psum_pool(name="ps", bufs=1))
+        ctx.enter_context(tc.manual_schedule())
+
+        words = sb.tile([P, 2, 2, 2 * M], U8, align_bytes=64)
+        wsc = sb.tile([P, 2, 2, M], U8, align_bytes=64)
+        warm_in = sb.tile([P, 8], F32)
+        warm_out = sb.tile([P, 8], F32)
+        grouped = sb.tile([P, 2 * N, 4], BF16, align_bytes=64)
+        codes = sb.tile([P, 2 * N], U32, align_bytes=64)
+        xsc = sb.tile([P, 2 * N], U8, align_bytes=64)
+        sig = sb.tile([P, 2, 2, N], F32, align_bytes=64)
+        res = sb.tile([P, 2, 2, N], F32, align_bytes=64)
+        raw = []
+        for k in range(len(LOADS)):
+            raw.append(sb.tile([P, 4, LOADS[k][1] - LOADS[k][0]], F32, name="raw%d" % k, align_bytes=64))
+        bank = []
+        for c in range(2):
+            bank.append([ps.tile([P, NT], F32, name="bank%d_%d" % (c, i)) for i in range(4)])
+
+        eng = {"v": nc.vector, "s": nc.scalar, "g": nc.gpsimd, "y": nc.sync}
+        wsrc = [w_words, u_words]
+        ssrc = [w_scales, u_scales]
+
+        def load_x(k):
+            c0, c1 = LOADS[k]
+            s = c0 // N
+            src = x[2 * s : 2 * s + 2].rearrange("c (p j) n -> (c p) j n", j=4)
+            nc.sync.dma_start(out=raw[k][:], in_=src[:, :, c0 - s * N : c1 - s * N])
+
+        def copy(e, c0, c1):
+            k = [i for i in range(len(LOADS)) if LOADS[i][0] <= c0 and c1 <= LOADS[i][1]][0]
+            o = LOADS[k][0]
+            if IL == 1:
+                dst = grouped[:, c0:c1, :]
+                src = raw[k][:, :, c0 - o : c1 - o].rearrange("p t c -> p c t")
+            else:
+                dst = grouped[:, c0:c1, :].rearrange("p (c i) t -> p c t i", i=IL)
+                src = raw[k][:, :, c0 - o : c1 - o].rearrange("p t (c i) -> p c t i", i=IL)
+            if e == "v":
+                nc.vector.tensor_copy(out=dst, in_=src)
+            elif e == "s":
+                nc.scalar.copy(out=dst, in_=src)
+            else:
+                nc.gpsimd.tensor_scalar(out=dst, in0=src, scalar1=1.0, scalar2=0.0, op0=ALU.mult, op1=ALU.add)
+
+        for step in PLAN:
+            op = step[0]
+            if op == "memset":
+                nc.vector.memset(wsc[:].rearrange("p a s m -> p (a s m)").bitcast(I32), 0)
+            elif op == "warm":
+                nc.vector.memset(warm_in[:], 0.0)
+                nc.scalar.activation(out=warm_out[:], in_=warm_in[:], func=ACT.Sigmoid)
+            elif op == "words":
+                e, a = step[1], step[2]
+                eng[e].dma_start(
+                    out=words[:, a, :, :].bitcast(I32),
+                    in_=wsrc[a].rearrange("(s c) p b -> (c p) s b", c=2).bitcast(I32),
+                )
+            elif op == "scales":
+                e, a, q = step[1], step[2], step[3]
+                eng[e].dma_start(
+                    out=wsc[32 * q : 32 * q + 4, a, :, :].bitcast(I32),
+                    in_=ssrc[a].rearrange("(s c) (h r) m -> (c h) r s m", c=2, r=4)[q].bitcast(I32),
+                )
+            elif op == "load":
+                load_x(step[1])
+            elif op == "copy":
+                copy(step[1], step[2], step[3])
+            elif op == "quant":
+                c0, c1 = step[1], step[2]
+                nc.vector.quantize_mx(
+                    out=codes[:, c0:c1].bitcast(FP8X4),
+                    scales=xsc[:, c0:c1],
+                    in_=grouped[:, c0:c1, :].rearrange("p c t -> p (c t)"),
+                )
+            elif op == "mm":
+                a, s, w0, b = step[1], step[2], step[3], step[4]
+                for c in range(2):
+                    r = slice(ROWS * c, ROWS * (c + 1))
+                    nc.tensor.matmul_mx(
+                        out=bank[c][b][:],
+                        lhsT=words[r, a, s, :].bitcast(FP4X4),
+                        lhsT_scale=wsc[r, a, s, :],
+                        rhs=codes[r, w0 : w0 + NT].bitcast(FP8X4),
+                        rhs_scale=xsc[r, w0 : w0 + NT],
+                        start=True,
+                        stop=True,
+                    )
+            elif op == "sig":
+                c, b, w0, c0, c1 = step[1:6]
+                s = c0 // N
+                nc.scalar.activation(
+                    out=sig[:, s, c, c0 - s * N : c1 - s * N], in_=bank[c][b][:, c0 - w0 : c1 - w0], func=ACT.Sigmoid
+                )
+            elif op == "mul":
+                c, b, w0, c0, c1 = step[1:6]
+                s = c0 // N
+                nc.vector.tensor_tensor(
+                    out=res[:, s, c, c0 - s * N : c1 - s * N],
+                    in0=bank[c][b][:, c0 - w0 : c1 - w0],
+                    in1=sig[:, s, c, c0 - s * N : c1 - s * N],
+                    op=ALU.mult,
+                )
+            elif op == "store":
+                e, ca, cb, c0, c1 = step[1:6]
+                s = c0 // N
+                eng[e].dma_start(
+                    out=out[2 * s + ca : 2 * s + cb, :, c0 - s * N : c1 - s * N].rearrange("c m n -> m c n"),
+                    in_=res[:, s, ca:cb, c0 - s * N : c1 - s * N],
+                )

@@ -20,21 +20,22 @@ ROWS = 64
 NT = 512
 LOADS = [[0,256],[256,512],[512,768],[768,1024],[1024,1280],[1280,1536],[1536,1792],[1792,2048]]
 IL = 4
-PLAN = [["memset"],
+PLAN = [["memset","v",0],
+    ["memset","v",1],
     ["words","s",0],
     ["words","s",1],
-    ["scales","s",0,0],
-    ["scales","s",0,1],
-    ["scales","s",0,2],
-    ["scales","s",0,3],
     ["load",0],
+    ["scales","y",0,0],
+    ["scales","y",0,1],
+    ["scales","y",0,2],
+    ["scales","y",0,3],
     ["load",1],
     ["warm"],
-    ["scales","s",1,0],
-    ["scales","s",1,1],
-    ["scales","s",1,2],
-    ["scales","s",1,3],
     ["load",2],
+    ["scales","y",1,0],
+    ["scales","y",1,1],
+    ["scales","y",1,2],
+    ["scales","y",1,3],
     ["load",3],
     ["load",4],
     ["load",5],
@@ -42,58 +43,66 @@ PLAN = [["memset"],
     ["load",7],
     ["copy","v",0,256],
     ["quant",0,256],
+    ["copy","s",736,768],
     ["copy","v",256,416],
     ["copy","s",416,512],
     ["quant",256,512],
-    ["mm",0,0,0,0],
-    ["mm",1,0,0,1],
-    ["copy","v",512,704],
-    ["copy","s",704,768],
+    ["mm1",0,0,0,0,1],
+    ["copy","v",512,736],
+    ["mm1",0,0,0,0,0],
     ["quant",512,768],
-    ["sig",0,0,0,0,512],
     ["sig",1,0,0,0,512],
-    ["mul",0,1,0,0,512],
-    ["copy","v",768,928],
-    ["copy","s",928,1024],
+    ["sig",0,0,0,0,512],
+    ["copy","s",1024,1280],
+    ["copy","v",768,1024],
+    ["copy","s",1280,1376],
+    ["mm1",1,0,0,1,1],
     ["quant",768,1024],
-    ["mm",0,0,512,2],
-    ["mm",1,0,512,3],
+    ["mm1",1,0,0,1,0],
     ["mul",1,1,0,0,512],
-    ["store","y",0,2,0,512],
-    ["copy","v",1024,1152],
-    ["copy","s",1152,1280],
-    ["quant",1024,1280],
+    ["mm1",0,0,512,2,0],
+    ["mul",0,1,0,0,512],
+    ["copy","v",1376,1536],
     ["sig",0,2,512,512,1024],
-    ["sig",1,2,512,512,1024],
-    ["mul",0,3,512,512,1024],
-    ["copy","v",1280,1440],
-    ["copy","s",1440,1536],
+    ["quant",1024,1280],
     ["quant",1280,1536],
-    ["mm",0,1,1024,0],
-    ["mm",1,1,1024,1],
-    ["mul",1,3,512,512,1024],
-    ["store","y",0,2,512,1024],
-    ["copy","v",1536,1664],
-    ["copy","s",1664,1792],
-    ["quant",1536,1792],
-    ["sig",0,0,1024,1024,1536],
-    ["copy","v",1792,1952],
+    ["mm1",1,0,512,3,0],
+    ["copy","v",1536,1792],
+    ["mm1",0,0,512,2,1],
+    ["mm1",1,0,512,3,1],
+    ["mul",0,3,512,512,1024],
+    ["sig",1,2,512,512,1024],
     ["copy","s",1952,2048],
-    ["mul",0,1,1024,1024,1536],
-    ["quant",1792,2048],
-    ["mm",0,1,1536,2],
-    ["mm",1,1,1536,3],
+    ["mm1",0,1,1024,0,0],
+    ["mm1",1,1,1024,1,0],
+    ["sig",0,0,1024,1024,1536],
+    ["mm1",0,1,1024,0,1],
+    ["store","y",1,2,0,512],
+    ["store","y",0,1,0,512],
+    ["copy","v",1792,1952],
+    ["quant",1536,1792],
+    ["store","y",0,1,512,1024],
     ["sig",1,0,1024,1024,1536],
+    ["mm1",1,1,1024,1,1],
+    ["quant",1792,2048],
+    ["mul",1,3,512,512,1024],
+    ["store","y",1,2,512,1024],
+    ["mul",0,1,1024,1024,1536],
+    ["mm1",0,1,1536,2,0],
+    ["mm1",1,1,1536,3,0],
+    ["mm1",0,1,1536,2,1],
     ["mul",1,1,1024,1024,1536],
-    ["store","y",0,2,1024,1536],
+    ["mm1",1,1,1536,3,1],
+    ["store","y",0,1,1024,1536],
+    ["store","y",1,2,1024,1536],
     ["sig",0,2,1536,1536,2048],
-    ["sig",1,2,1536,1536,1792],
-    ["sig",1,2,1536,1792,2048],
     ["mul",0,3,1536,1536,2048],
+    ["sig",1,2,1536,1536,1792],
     ["store","y",0,1,1536,2048],
     ["mul",1,3,1536,1536,1792],
-    ["store","y",1,2,1536,1792],
+    ["sig",1,2,1536,1792,2048],
     ["mul",1,3,1536,1792,2048],
+    ["store","y",1,2,1536,1792],
     ["store","y",1,2,1792,2048]]
 
 
@@ -104,8 +113,8 @@ def tile_rows_gglu_sigmoid_kernel(tc, x, w_words, w_scales, u_words, u_scales, o
         ps = ctx.enter_context(tc.psum_pool(name="ps", bufs=1))
         ctx.enter_context(tc.manual_schedule())
 
-        words = sb.tile([P, 2, 2, 2 * M], U8, align_bytes=64)
-        wsc = sb.tile([P, 2, 2, M], U8, align_bytes=64)
+        words = [sb.tile([P, 2, 2 * M], U8, name="words%d" % a, align_bytes=64) for a in range(2)]
+        wsc = [sb.tile([P, 2, M], U8, name="wsc%d" % a, align_bytes=64) for a in range(2)]
         warm_in = sb.tile([P, 8], F32)
         warm_out = sb.tile([P, 8], F32)
         grouped = sb.tile([P, 2 * N, 4], BF16, align_bytes=64)
@@ -149,20 +158,20 @@ def tile_rows_gglu_sigmoid_kernel(tc, x, w_words, w_scales, u_words, u_scales, o
         for step in PLAN:
             op = step[0]
             if op == "memset":
-                nc.vector.memset(wsc[:].rearrange("p a s m -> p (a s m)").bitcast(I32), 0)
+                eng[step[1]].memset(wsc[step[2]][:].rearrange("p s m -> p (s m)").bitcast(I32), 0)
             elif op == "warm":
                 nc.vector.memset(warm_in[:], 0.0)
                 nc.scalar.activation(out=warm_out[:], in_=warm_in[:], func=ACT.Sigmoid)
             elif op == "words":
                 e, a = step[1], step[2]
                 eng[e].dma_start(
-                    out=words[:, a, :, :].bitcast(I32),
+                    out=words[a][:].bitcast(I32),
                     in_=wsrc[a].rearrange("(s c) p b -> (c p) s b", c=2).bitcast(I32),
                 )
             elif op == "scales":
                 e, a, q = step[1], step[2], step[3]
                 eng[e].dma_start(
-                    out=wsc[32 * q : 32 * q + 4, a, :, :].bitcast(I32),
+                    out=wsc[a][32 * q : 32 * q + 4, :, :].bitcast(I32),
                     in_=ssrc[a].rearrange("(s c) (h r) m -> (c h) r s m", c=2, r=4)[q].bitcast(I32),
                 )
             elif op == "load":
@@ -182,13 +191,25 @@ def tile_rows_gglu_sigmoid_kernel(tc, x, w_words, w_scales, u_words, u_scales, o
                     r = slice(ROWS * c, ROWS * (c + 1))
                     nc.tensor.matmul_mx(
                         out=bank[c][b][:],
-                        lhsT=words[r, a, s, :].bitcast(FP4X4),
-                        lhsT_scale=wsc[r, a, s, :],
+                        lhsT=words[a][r, s, :].bitcast(FP4X4),
+                        lhsT_scale=wsc[a][r, s, :],
                         rhs=codes[r, w0 : w0 + NT].bitcast(FP8X4),
                         rhs_scale=xsc[r, w0 : w0 + NT],
                         start=True,
                         stop=True,
                     )
+            elif op == "mm1":
+                a, s, w0, b, c = step[1:6]
+                r = slice(ROWS * c, ROWS * (c + 1))
+                nc.tensor.matmul_mx(
+                    out=bank[c][b][:],
+                    lhsT=words[a][r, s, :].bitcast(FP4X4),
+                    lhsT_scale=wsc[a][r, s, :],
+                    rhs=codes[r, w0 : w0 + NT].bitcast(FP8X4),
+                    rhs_scale=xsc[r, w0 : w0 + NT],
+                    start=True,
+                    stop=True,
+                )
             elif op == "sig":
                 c, b, w0, c0, c1 = step[1:6]
                 s = c0 // N

@@ -22,15 +22,15 @@ LOADS = [[0,256],[256,512],[512,768],[768,1024],[1024,1280],[1280,1536],[1536,17
 IL = 4
 PLAN = [["memset","v",0],
     ["memset","v",1],
-    ["words","s",0],
-    ["words","s",1],
+    ["warm"],
+    ["words","y",0],
     ["load",0],
     ["scales","y",0,0],
     ["scales","y",0,1],
     ["scales","y",0,2],
     ["scales","y",0,3],
     ["load",1],
-    ["warm"],
+    ["words","y",1],
     ["load",2],
     ["scales","y",1,0],
     ["scales","y",1,1],
@@ -43,66 +43,66 @@ PLAN = [["memset","v",0],
     ["load",7],
     ["copy","v",0,256],
     ["quant",0,256],
-    ["copy","s",736,768],
     ["copy","v",256,416],
     ["copy","s",416,512],
     ["quant",256,512],
-    ["mm1",0,0,0,0,1],
-    ["copy","v",512,736],
     ["mm1",0,0,0,0,0],
-    ["quant",512,768],
-    ["sig",1,0,0,0,512],
-    ["sig",0,0,0,0,512],
-    ["copy","s",1024,1280],
-    ["copy","v",768,1024],
-    ["copy","s",1280,1376],
-    ["mm1",1,0,0,1,1],
-    ["quant",768,1024],
+    ["mm1",0,0,0,0,1],
     ["mm1",1,0,0,1,0],
-    ["mul",1,1,0,0,512],
+    ["mm1",1,0,0,1,1],
+    ["copy","v",512,768],
+    ["quant",512,768],
+    ["sig",0,0,0,0,512],
+    ["copy","v",768,1024],
+    ["sig",1,0,0,0,512],
+    ["quant",768,1024],
     ["mm1",0,0,512,2,0],
+    ["mm1",0,0,512,2,1],
+    ["mm1",1,0,512,3,0],
+    ["mm1",1,0,512,3,1],
     ["mul",0,1,0,0,512],
-    ["copy","v",1376,1536],
-    ["sig",0,2,512,512,1024],
+    ["mul",1,1,0,0,512],
+    ["store","y",0,1,0,512],
+    ["store","y",1,2,0,512],
+    ["copy","s",1024,1280],
+    ["copy","v",1280,1440],
+    ["copy","s",1440,1536],
     ["quant",1024,1280],
     ["quant",1280,1536],
-    ["mm1",1,0,512,3,0],
-    ["copy","v",1536,1792],
-    ["mm1",0,0,512,2,1],
-    ["mm1",1,0,512,3,1],
-    ["mul",0,3,512,512,1024],
-    ["sig",1,2,512,512,1024],
-    ["copy","s",1952,2048],
     ["mm1",0,1,1024,0,0],
-    ["mm1",1,1,1024,1,0],
-    ["sig",0,0,1024,1024,1536],
     ["mm1",0,1,1024,0,1],
-    ["store","y",1,2,0,512],
-    ["store","y",0,1,0,512],
-    ["copy","v",1792,1952],
-    ["quant",1536,1792],
-    ["store","y",0,1,512,1024],
-    ["sig",1,0,1024,1024,1536],
+    ["mm1",1,1,1024,1,0],
     ["mm1",1,1,1024,1,1],
+    ["sig",0,2,512,512,1024],
+    ["sig",1,2,512,512,1024],
+    ["mul",0,3,512,512,1024],
+    ["store","y",0,1,512,1024],
+    ["copy","v",1536,1664],
+    ["copy","s",1664,1792],
+    ["copy","v",1792,1952],
+    ["copy","s",1952,2048],
+    ["quant",1536,1792],
     ["quant",1792,2048],
-    ["mul",1,3,512,512,1024],
-    ["store","y",1,2,512,1024],
-    ["mul",0,1,1024,1024,1536],
+    ["sig",0,0,1024,1024,1536],
+    ["sig",1,0,1024,1024,1536],
     ["mm1",0,1,1536,2,0],
+    ["mul",1,3,512,512,1024],
     ["mm1",1,1,1536,3,0],
     ["mm1",0,1,1536,2,1],
-    ["mul",1,1,1024,1024,1536],
     ["mm1",1,1,1536,3,1],
+    ["store","y",1,2,512,1024],
+    ["mul",0,1,1024,1024,1536],
     ["store","y",0,1,1024,1536],
+    ["mul",1,1,1024,1024,1536],
     ["store","y",1,2,1024,1536],
     ["sig",0,2,1536,1536,2048],
-    ["mul",0,3,1536,1536,2048],
     ["sig",1,2,1536,1536,1792],
+    ["sig",1,2,1536,1792,2048],
+    ["mul",0,3,1536,1536,2048],
     ["store","y",0,1,1536,2048],
     ["mul",1,3,1536,1536,1792],
-    ["sig",1,2,1536,1792,2048],
-    ["mul",1,3,1536,1792,2048],
     ["store","y",1,2,1536,1792],
+    ["mul",1,3,1536,1792,2048],
     ["store","y",1,2,1792,2048]]
 
 

@@ -18,7 +18,7 @@ ALU = mybir.AluOpType
 P = 128
 ROWS = 64
 NT = 512
-LOADS = [[0,256],[256,512],[512,768],[768,1024],[1024,1280],[1280,1536],[1536,1792],[1792,2048]]
+LOADS = [[0,512],[512,1024],[1024,1536],[1536,1792],[1792,2048]]
 IL = 4
 PLAN = [["memset","v",0],
     ["memset","v",1],
@@ -29,79 +29,73 @@ PLAN = [["memset","v",0],
     ["scales","y",0,1],
     ["scales","y",0,2],
     ["scales","y",0,3],
-    ["load",1],
     ["words","y",1],
-    ["load",2],
+    ["load",1],
     ["scales","y",1,0],
     ["scales","y",1,1],
     ["scales","y",1,2],
     ["scales","y",1,3],
+    ["load",2],
     ["load",3],
     ["load",4],
-    ["load",5],
-    ["load",6],
-    ["load",7],
-    ["copy","v",0,256],
+    ["copy","v",0,352],
+    ["copy","s",352,512],
     ["quant",0,256],
-    ["copy","v",256,416],
-    ["copy","s",416,512],
     ["quant",256,512],
     ["mm1",0,0,0,0,0],
-    ["mm1",0,0,0,0,1],
     ["mm1",1,0,0,1,0],
+    ["mm1",0,0,0,0,1],
     ["mm1",1,0,0,1,1],
-    ["copy","v",512,768],
+    ["copy","v",512,864],
+    ["copy","s",864,1024],
     ["quant",512,768],
-    ["sig",0,0,0,0,512],
-    ["copy","v",768,1024],
-    ["sig",1,0,0,0,512],
     ["quant",768,1024],
     ["mm1",0,0,512,2,0],
-    ["mm1",0,0,512,2,1],
     ["mm1",1,0,512,3,0],
+    ["mm1",0,0,512,2,1],
     ["mm1",1,0,512,3,1],
+    ["sig",0,0,0,0,512],
+    ["sig",1,0,0,0,512],
     ["mul",0,1,0,0,512],
-    ["mul",1,1,0,0,512],
     ["store","y",0,1,0,512],
-    ["store","y",1,2,0,512],
-    ["copy","s",1024,1280],
-    ["copy","v",1280,1440],
-    ["copy","s",1440,1536],
+    ["copy","v",1024,1312],
+    ["copy","s",1312,1536],
     ["quant",1024,1280],
     ["quant",1280,1536],
+    ["mul",1,1,0,0,512],
+    ["store","y",1,2,0,512],
     ["mm1",0,1,1024,0,0],
-    ["mm1",0,1,1024,0,1],
     ["mm1",1,1,1024,1,0],
+    ["mm1",0,1,1024,0,1],
     ["mm1",1,1,1024,1,1],
     ["sig",0,2,512,512,1024],
-    ["sig",1,2,512,512,1024],
     ["mul",0,3,512,512,1024],
     ["store","y",0,1,512,1024],
-    ["copy","v",1536,1664],
-    ["copy","s",1664,1792],
-    ["copy","v",1792,1952],
-    ["copy","s",1952,2048],
+    ["copy","s",1536,1792],
+    ["copy","v",1792,1984],
+    ["copy","s",1984,2048],
     ["quant",1536,1792],
     ["quant",1792,2048],
-    ["sig",0,0,1024,1024,1536],
-    ["sig",1,0,1024,1024,1536],
-    ["mm1",0,1,1536,2,0],
+    ["sig",1,2,512,512,1024],
     ["mul",1,3,512,512,1024],
+    ["store","y",1,2,512,1024],
+    ["mm1",0,1,1536,2,0],
     ["mm1",1,1,1536,3,0],
     ["mm1",0,1,1536,2,1],
     ["mm1",1,1,1536,3,1],
-    ["store","y",1,2,512,1024],
+    ["sig",0,0,1024,1024,1536],
     ["mul",0,1,1024,1024,1536],
     ["store","y",0,1,1024,1536],
+    ["sig",1,0,1024,1024,1536],
     ["mul",1,1,1024,1024,1536],
     ["store","y",1,2,1024,1536],
     ["sig",0,2,1536,1536,2048],
-    ["sig",1,2,1536,1536,1792],
-    ["sig",1,2,1536,1792,2048],
     ["mul",0,3,1536,1536,2048],
     ["store","y",0,1,1536,2048],
+    ["sig",1,2,1536,1536,1792],
     ["mul",1,3,1536,1536,1792],
     ["store","y",1,2,1536,1792],
+    ["sig",1,2,1536,1792,2048],
     ["mul",1,3,1536,1792,2048],
     ["store","y",1,2,1792,2048]]
 

@@ -19,85 +19,6 @@ P = 128
 ROWS = 64
 NT = 512
 LOADS = [[0,512],[512,1024],[1024,1536],[1536,1792],[1792,2048]]
-IL = 4
-PLAN = [["memset","v",0],
-    ["memset","v",1],
-    ["warm"],
-    ["words","y",0],
-    ["load",0],
-    ["scales","y",0,0],
-    ["scales","y",0,1],
-    ["scales","y",0,2],
-    ["scales","y",0,3],
-    ["words","y",1],
-    ["load",1],
-    ["scales","y",1,0],
-    ["scales","y",1,1],
-    ["scales","y",1,2],
-    ["scales","y",1,3],
-    ["load",2],
-    ["load",3],
-    ["load",4],
-    ["copy","v",0,352],
-    ["copy","s",352,512],
-    ["quant",0,256],
-    ["quant",256,512],
-    ["mm1",0,0,0,0,0],
-    ["mm1",1,0,0,1,0],
-    ["mm1",0,0,0,0,1],
-    ["mm1",1,0,0,1,1],
-    ["copy","v",512,864],
-    ["copy","s",864,1024],
-    ["quant",512,768],
-    ["quant",768,1024],
-    ["mm1",0,0,512,2,0],
-    ["mm1",1,0,512,3,0],
-    ["mm1",0,0,512,2,1],
-    ["mm1",1,0,512,3,1],
-    ["sig",0,0,0,0,512],
-    ["sig",1,0,0,0,512],
-    ["mul",0,1,0,0,512],
-    ["store","y",0,1,0,512],
-    ["copy","v",1024,1312],
-    ["copy","s",1312,1536],
-    ["quant",1024,1280],
-    ["quant",1280,1536],
-    ["mul",1,1,0,0,512],
-    ["store","y",1,2,0,512],
-    ["mm1",0,1,1024,0,0],
-    ["mm1",1,1,1024,1,0],
-    ["mm1",0,1,1024,0,1],
-    ["mm1",1,1,1024,1,1],
-    ["sig",0,2,512,512,1024],
-    ["mul",0,3,512,512,1024],
-    ["store","y",0,1,512,1024],
-    ["copy","s",1536,1792],
-    ["copy","v",1792,1984],
-    ["copy","s",1984,2048],
-    ["quant",1536,1792],
-    ["quant",1792,2048],
-    ["sig",1,2,512,512,1024],
-    ["mul",1,3,512,512,1024],
-    ["store","y",1,2,512,1024],
-    ["mm1",0,1,1536,2,0],
-    ["mm1",1,1,1536,3,0],
-    ["mm1",0,1,1536,2,1],
-    ["mm1",1,1,1536,3,1],
-    ["sig",0,0,1024,1024,1536],
-    ["mul",0,1,1024,1024,1536],
-    ["store","y",0,1,1024,1536],
-    ["sig",1,0,1024,1024,1536],
-    ["mul",1,1,1024,1024,1536],
-    ["store","y",1,2,1024,1536],
-    ["sig",0,2,1536,1536,2048],
-    ["mul",0,3,1536,1536,2048],
-    ["store","y",0,1,1536,2048],
-    ["sig",1,2,1536,1536,1792],
-    ["mul",1,3,1536,1536,1792],
-    ["store","y",1,2,1536,1792],
-    ["sig",1,2,1536,1792,2048],
-    ["mul",1,3,1536,1792,2048],
-    ["store","y",1,2,1792,2048]]
 
 
 def tile_rows_gglu_sigmoid_kernel(tc, x, w_words, w_scales, u_words, u_scales, out):
@@ -114,77 +35,65 @@ def tile_rows_gglu_sigmoid_kernel(tc, x, w_words, w_scales, u_words, u_scales, o
         grouped = sb.tile([P, 2 * N, 4], BF16, align_bytes=64)
         codes = sb.tile([P, 2 * N], U32, align_bytes=64)
         xsc = sb.tile([P, 2 * N], U8, align_bytes=64)
-        sig = sb.tile([P, 2, 2, N], F32, align_bytes=64)
-        res = sb.tile([P, 2, 2, N], F32, align_bytes=64)
-        raw = []
-        for k in range(len(LOADS)):
-            raw.append(sb.tile([P, 4, LOADS[k][1] - LOADS[k][0]], F32, name="raw%d" % k, align_bytes=64))
-        bank = []
-        for c in range(2):
-            bank.append([ps.tile([P, NT], F32, name="bank%d_%d" % (c, i)) for i in range(4)])
-
-        eng = {"v": nc.vector, "s": nc.scalar, "g": nc.gpsimd, "y": nc.sync}
+        sig = sb.tile([P, 2, 2 * N], F32, align_bytes=64)
+        res = sb.tile([P, 2, 2 * N], F32, align_bytes=64)
+        raw = [sb.tile([P, 4, hi - lo], F32, name="raw%d" % lo, align_bytes=64) for lo, hi in LOADS]
+        bank = [[ps.tile([P, NT], F32, name="bank%d_%d" % (c, i)) for i in range(4)] for c in range(2)]
         wsrc = [w_words, u_words]
         ssrc = [w_scales, u_scales]
 
-        def load_x(k):
-            c0, c1 = LOADS[k]
-            s = c0 // N
-            src = x[2 * s : 2 * s + 2].rearrange("c (p j) n -> (c p) j n", j=4)
-            nc.sync.dma_start(out=raw[k][:], in_=src[:, :, c0 - s * N : c1 - s * N])
+        def load_words(eng, a):
+            eng.dma_start(
+                out=words[a][:].bitcast(I32),
+                in_=wsrc[a].rearrange("(s c) p b -> (c p) s b", c=2).bitcast(I32),
+            )
 
-        def copy(e, c0, c1):
-            k = [i for i in range(len(LOADS)) if LOADS[i][0] <= c0 and c1 <= LOADS[i][1]][0]
-            o = LOADS[k][0]
-            if IL == 1:
-                dst = grouped[:, c0:c1, :]
-                src = raw[k][:, :, c0 - o : c1 - o].rearrange("p t c -> p c t")
-            else:
-                dst = grouped[:, c0:c1, :].rearrange("p (c i) t -> p c t i", i=IL)
-                src = raw[k][:, :, c0 - o : c1 - o].rearrange("p t (c i) -> p c t i", i=IL)
-            if e == "v":
-                nc.vector.tensor_copy(out=dst, in_=src)
-            elif e == "s":
-                nc.scalar.copy(out=dst, in_=src)
-            else:
-                nc.gpsimd.tensor_scalar(out=dst, in0=src, scalar1=1.0, scalar2=0.0, op0=ALU.mult, op1=ALU.add)
-
-        for step in PLAN:
-            op = step[0]
-            if op == "memset":
-                eng[step[1]].memset(wsc[step[2]][:].rearrange("p s m -> p (s m)").bitcast(I32), 0)
-            elif op == "warm":
-                nc.vector.memset(warm_in[:], 0.0)
-                nc.scalar.activation(out=warm_out[:], in_=warm_in[:], func=ACT.Sigmoid)
-            elif op == "words":
-                e, a = step[1], step[2]
-                eng[e].dma_start(
-                    out=words[a][:].bitcast(I32),
-                    in_=wsrc[a].rearrange("(s c) p b -> (c p) s b", c=2).bitcast(I32),
-                )
-            elif op == "scales":
-                e, a, q = step[1], step[2], step[3]
-                eng[e].dma_start(
+        def load_scales(eng, a):
+            for q in range(4):
+                eng.dma_start(
                     out=wsc[a][32 * q : 32 * q + 4, :, :].bitcast(I32),
                     in_=ssrc[a].rearrange("(s c) (h r) m -> (c h) r s m", c=2, r=4)[q].bitcast(I32),
                 )
-            elif op == "load":
-                load_x(step[1])
-            elif op == "copy":
-                copy(step[1], step[2], step[3])
-            elif op == "quant":
-                c0, c1 = step[1], step[2]
-                nc.vector.quantize_mx(
-                    out=codes[:, c0:c1].bitcast(FP8X4),
-                    scales=xsc[:, c0:c1],
-                    in_=grouped[:, c0:c1, :].rearrange("p c t -> p (c t)"),
-                )
-            elif op == "mm":
-                a, s, w0, b = step[1], step[2], step[3], step[4]
+
+        def load_x(k, eng=nc.sync):
+            lo, hi = LOADS[k]
+            s = lo // N
+            src = x[2 * s : 2 * s + 2].rearrange("c (p j) n -> (c p) j n", j=4)
+            eng.dma_start(out=raw[k][:], in_=src[:, :, lo - s * N : hi - s * N])
+
+        def views(lo, hi):
+            k = [i for i in range(len(LOADS)) if LOADS[i][0] <= lo and hi <= LOADS[i][1]][0]
+            o = LOADS[k][0]
+            dst = grouped[:, lo:hi, :].rearrange("p (c i) t -> p c t i", i=4)
+            src = raw[k][:, :, lo - o : hi - o].rearrange("p t (c i) -> p c t i", i=4)
+            return dst, src
+
+        def copy_v(lo, hi):
+            dst, src = views(lo, hi)
+            nc.vector.tensor_copy(out=dst, in_=src)
+
+        def copy_s(lo, hi):
+            dst, src = views(lo, hi)
+            nc.scalar.copy(out=dst, in_=src)
+
+        def copy_g(lo, hi):
+            dst, src = views(lo, hi)
+            nc.gpsimd.tensor_scalar(out=dst, in0=src, scalar1=1.0, scalar2=0.0, op0=ALU.mult, op1=ALU.add)
+
+        def quant(lo, hi):
+            nc.vector.quantize_mx(
+                out=codes[:, lo:hi].bitcast(FP8X4),
+                scales=xsc[:, lo:hi],
+                in_=grouped[:, lo:hi, :].rearrange("p c t -> p (c t)"),
+            )
+
+        def matmuls(w0, slot):
+            s = w0 // N
+            for a in range(2):
                 for c in range(2):
                     r = slice(ROWS * c, ROWS * (c + 1))
                     nc.tensor.matmul_mx(
-                        out=bank[c][b][:],
+                        out=bank[c][2 * slot + a][:],
                         lhsT=words[a][r, s, :].bitcast(FP4X4),
                         lhsT_scale=wsc[a][r, s, :],
                         rhs=codes[r, w0 : w0 + NT].bitcast(FP8X4),
@@ -192,37 +101,74 @@ def tile_rows_gglu_sigmoid_kernel(tc, x, w_words, w_scales, u_words, u_scales, o
                         start=True,
                         stop=True,
                     )
-            elif op == "mm1":
-                a, s, w0, b, c = step[1:6]
-                r = slice(ROWS * c, ROWS * (c + 1))
-                nc.tensor.matmul_mx(
-                    out=bank[c][b][:],
-                    lhsT=words[a][r, s, :].bitcast(FP4X4),
-                    lhsT_scale=wsc[a][r, s, :],
-                    rhs=codes[r, w0 : w0 + NT].bitcast(FP8X4),
-                    rhs_scale=xsc[r, w0 : w0 + NT],
-                    start=True,
-                    stop=True,
-                )
-            elif op == "sig":
-                c, b, w0, c0, c1 = step[1:6]
-                s = c0 // N
-                nc.scalar.activation(
-                    out=sig[:, s, c, c0 - s * N : c1 - s * N], in_=bank[c][b][:, c0 - w0 : c1 - w0], func=ACT.Sigmoid
-                )
-            elif op == "mul":
-                c, b, w0, c0, c1 = step[1:6]
-                s = c0 // N
-                nc.vector.tensor_tensor(
-                    out=res[:, s, c, c0 - s * N : c1 - s * N],
-                    in0=bank[c][b][:, c0 - w0 : c1 - w0],
-                    in1=sig[:, s, c, c0 - s * N : c1 - s * N],
-                    op=ALU.mult,
-                )
-            elif op == "store":
-                e, ca, cb, c0, c1 = step[1:6]
-                s = c0 // N
-                eng[e].dma_start(
-                    out=out[2 * s + ca : 2 * s + cb, :, c0 - s * N : c1 - s * N].rearrange("c m n -> m c n"),
-                    in_=res[:, s, ca:cb, c0 - s * N : c1 - s * N],
-                )
+
+        def sigmoid(c, w0, slot, lo, hi):
+            nc.scalar.activation(out=sig[:, c, lo:hi], in_=bank[c][2 * slot][:, lo - w0 : hi - w0], func=ACT.Sigmoid)
+
+        def gate(c, w0, slot, lo, hi):
+            nc.vector.tensor_tensor(
+                out=res[:, c, lo:hi], in0=bank[c][2 * slot + 1][:, lo - w0 : hi - w0], in1=sig[:, c, lo:hi], op=ALU.mult
+            )
+
+        def store(c, lo, hi, eng=nc.sync):
+            s = lo // N
+            eng.dma_start(out=out[2 * s + c, :, lo - s * N : hi - s * N], in_=res[:, c, lo:hi])
+
+        for a in range(2):
+            nc.vector.memset(wsc[a][:].rearrange("p s m -> p (s m)").bitcast(I32), 0)
+        nc.vector.memset(warm_in[:], 0.0)
+        nc.scalar.activation(out=warm_out[:], in_=warm_in[:], func=ACT.Sigmoid)
+        load_x(0)
+        load_scales(nc.sync, 0)
+        load_x(1)
+        load_words(nc.sync, 0)
+        load_words(nc.sync, 1)
+        load_scales(nc.sync, 1)
+        for k in range(2, len(LOADS)):
+            load_x(k)
+
+        def sg(u, c, lo=0, hi=NT):
+            sigmoid(c, u * NT, u % 2, u * NT + lo, u * NT + hi)
+
+        def gt(u, c, lo=0, hi=NT):
+            gate(c, u * NT, u % 2, u * NT + lo, u * NT + hi)
+            store(c, u * NT + lo, u * NT + hi)
+
+        def q2(u):
+            quant(u * NT, u * NT + 256)
+            quant(u * NT + 256, u * NT + NT)
+
+        for u in range(2):
+            copy_v(u * NT, u * NT + 320)
+            copy_s(u * NT + 320, u * NT + NT)
+            q2(u)
+        matmuls(0, 0)
+        matmuls(NT, 1)
+        sg(0, 0)
+        sg(0, 1)
+        sg(1, 0)
+        gt(0, 0)
+        gt(0, 1)
+        copy_v(1024, 1024 + 320)
+        copy_s(1024 + 320, 1536)
+        gt(1, 0)
+        q2(2)
+        matmuls(1024, 0)
+        sg(1, 1)
+        gt(1, 1)
+        copy_s(1536, 1792)
+        copy_v(1792, 1792 + 192)
+        copy_s(1792 + 192, 2048)
+        q2(3)
+        matmuls(1536, 1)
+        for c in range(2):
+            sg(2, c)
+            gt(2, c)
+        sg(3, 0, 0, 256)
+        sg(3, 0, 256, 512)
+        gate(0, 1536, 1, 1536, 1792)
+        gate(0, 1536, 1, 1792, 2048)
+        store(0, 1536, 2048)
+        for lo in (0, 256):
+            sg(3, 1, lo, lo + 256)
+            gt(3, 1, lo, lo + 256)

@@ -18,7 +18,8 @@ ALU = mybir.AluOpType
 P = 128
 ROWS = 64
 NT = 512
-LOADS = [[0,512],[512,1024],[1024,1536],[1536,1792],[1792,2048]]
+LOADS = [[0,512],[512,1024],[1024,1408],[1408,1792],[1792,2048]]
+BANKS = [[0,1],[2,3],[0,1],[2,3],[0,1]]
 
 
 def tile_rows_gglu_sigmoid_kernel(tc, x, w_words, w_scales, u_words, u_scales, out):
@@ -87,28 +88,56 @@ def tile_rows_gglu_sigmoid_kernel(tc, x, w_words, w_scales, u_words, u_scales, o
                 in_=grouped[:, lo:hi, :].rearrange("p c t -> p (c t)"),
             )
 
-        def matmuls(w0, slot):
-            s = w0 // N
-            for a in range(2):
-                for c in range(2):
-                    r = slice(ROWS * c, ROWS * (c + 1))
-                    nc.tensor.matmul_mx(
-                        out=bank[c][2 * slot + a][:],
-                        lhsT=words[a][r, s, :].bitcast(FP4X4),
-                        lhsT_scale=wsc[a][r, s, :],
-                        rhs=codes[r, w0 : w0 + NT].bitcast(FP8X4),
-                        rhs_scale=xsc[r, w0 : w0 + NT],
-                        start=True,
-                        stop=True,
-                    )
+        def product(a, k):
+            lo, hi = LOADS[k]
+            s = lo // N
+            for c in range(2):
+                r = slice(ROWS * c, ROWS * (c + 1))
+                nc.tensor.matmul_mx(
+                    out=bank[c][BANKS[k][a]][:],
+                    lhsT=words[a][r, s, :].bitcast(FP4X4),
+                    lhsT_scale=wsc[a][r, s, :],
+                    rhs=codes[r, hi - NT : hi].bitcast(FP8X4),
+                    rhs_scale=xsc[r, hi - NT : hi],
+                    start=True,
+                    stop=True,
+                )
 
-        def sigmoid(c, w0, slot, lo, hi):
-            nc.scalar.activation(out=sig[:, c, lo:hi], in_=bank[c][2 * slot][:, lo - w0 : hi - w0], func=ACT.Sigmoid)
+        def mm(k):
+            product(0, k)
+            product(1, k)
 
-        def gate(c, w0, slot, lo, hi):
+        def sg(k, c):
+            lo, hi = LOADS[k]
+            nc.scalar.activation(out=sig[:, c, lo:hi], in_=bank[c][BANKS[k][0]][:, NT - (hi - lo) :], func=ACT.Sigmoid)
+
+        def gt(k, c):
+            lo, hi = LOADS[k]
             nc.vector.tensor_tensor(
-                out=res[:, c, lo:hi], in0=bank[c][2 * slot + 1][:, lo - w0 : hi - w0], in1=sig[:, c, lo:hi], op=ALU.mult
+                out=res[:, c, lo:hi], in0=bank[c][BANKS[k][1]][:, NT - (hi - lo) :], in1=sig[:, c, lo:hi], op=ALU.mult
             )
+
+        def st(k, c):
+            store(c, LOADS[k][0], LOADS[k][1])
+
+        def st2(k):
+            lo, hi = LOADS[k]
+            s = lo // N
+            nc.sync.dma_start(
+                out=out[2 * s : 2 * s + 2, :, lo - s * N : hi - s * N].rearrange("c m n -> m c n"), in_=res[:, :, lo:hi]
+            )
+
+        def cp(k, v):
+            lo, hi = LOADS[k]
+            if v > 0:
+                copy_v(lo, lo + v)
+            if lo + v < hi:
+                copy_s(lo + v, hi)
+
+        def qq(k):
+            lo, hi = LOADS[k]
+            for a in range(lo, hi, 256):
+                quant(a, min(a + 256, hi))
 
         def store(c, lo, hi, eng=nc.sync):
             s = lo // N
@@ -118,57 +147,48 @@ def tile_rows_gglu_sigmoid_kernel(tc, x, w_words, w_scales, u_words, u_scales, o
             nc.vector.memset(wsc[a][:].rearrange("p s m -> p (s m)").bitcast(I32), 0)
         nc.vector.memset(warm_in[:], 0.0)
         nc.scalar.activation(out=warm_out[:], in_=warm_in[:], func=ACT.Sigmoid)
+        def words_pair(a, s):
+            nc.sync.dma_start(
+                out=words[a][:, s, :].bitcast(I32),
+                in_=wsrc[a][2 * s : 2 * s + 2].rearrange("c p b -> (c p) b").bitcast(I32),
+            )
+
         load_x(0)
         load_scales(nc.sync, 0)
         load_x(1)
-        load_words(nc.sync, 0)
-        load_words(nc.sync, 1)
+        words_pair(0, 0)
+        words_pair(1, 0)
         load_scales(nc.sync, 1)
-        for k in range(2, len(LOADS)):
-            load_x(k)
+        load_x(2)
+        words_pair(0, 1)
+        words_pair(1, 1)
+        load_x(3)
+        load_x(4)
+        SHARE = [320,384,192,192,128]
+        last = len(LOADS) - 1
 
-        def sg(u, c, lo=0, hi=NT):
-            sigmoid(c, u * NT, u % 2, u * NT + lo, u * NT + hi)
+        def out_of(k, c):
+            gt(k, c)
+            st(k, c)
 
-        def gt(u, c, lo=0, hi=NT):
-            gate(c, u * NT, u % 2, u * NT + lo, u * NT + hi)
-            store(c, u * NT + lo, u * NT + hi)
-
-        def q2(u):
-            quant(u * NT, u * NT + 256)
-            quant(u * NT + 256, u * NT + NT)
-
-        for u in range(2):
-            copy_v(u * NT, u * NT + 320)
-            copy_s(u * NT + 320, u * NT + NT)
-            q2(u)
-        matmuls(0, 0)
-        matmuls(NT, 1)
-        sg(0, 0)
-        sg(0, 1)
-        sg(1, 0)
-        gt(0, 0)
-        gt(0, 1)
-        copy_v(1024, 1024 + 320)
-        copy_s(1024 + 320, 1536)
-        gt(1, 0)
-        q2(2)
-        matmuls(1024, 0)
-        sg(1, 1)
-        gt(1, 1)
-        copy_s(1536, 1792)
-        copy_v(1792, 1792 + 192)
-        copy_s(1792 + 192, 2048)
-        q2(3)
-        matmuls(1536, 1)
-        for c in range(2):
-            sg(2, c)
-            gt(2, c)
-        sg(3, 0, 0, 256)
-        sg(3, 0, 256, 512)
-        gate(0, 1536, 1, 1536, 1792)
-        gate(0, 1536, 1, 1792, 2048)
-        store(0, 1536, 2048)
-        for lo in (0, 256):
-            sg(3, 1, lo, lo + 256)
-            gt(3, 1, lo, lo + 256)
+        for k in range(last):
+            cp(k, SHARE[k])
+            if k >= 1:
+                sg(k - 1, 0)
+            if k >= 2:
+                out_of(k - 2, 1)
+            qq(k)
+            mm(k)
+            if 1 <= k < last - 1:
+                sg(k - 1, 1)
+                out_of(k - 1, 0)
+        cp(last, SHARE[last])
+        sg(last - 2, 1)
+        out_of(last - 2, 0)
+        qq(last)
+        out_of(last - 2, 1)
+        mm(last)
+        for k in (last - 1, last):
+            for c in range(2):
+                sg(k, c)
+                out_of(k, c)

@@ -29,16 +29,16 @@ def tile_rows_gglu_sigmoid_kernel(tc, x, w_words, w_scales, u_words, u_scales, o
         ps = ctx.enter_context(tc.psum_pool(name="ps", bufs=1))
         ctx.enter_context(tc.manual_schedule())
 
-        words = [sb.tile([P, 2, 2 * M], U8, name="words%d" % a, align_bytes=64) for a in range(2)]
-        wsc = [sb.tile([P, 2, M], U8, name="wsc%d" % a, align_bytes=64) for a in range(2)]
+        words = [sb.tile([P, 2, 2 * M], U8, name="words%d" % a, align_bytes=256) for a in range(2)]
+        wsc = [sb.tile([P, 2, M], U8, name="wsc%d" % a, align_bytes=256) for a in range(2)]
         warm_in = sb.tile([P, 8], F32)
         warm_out = sb.tile([P, 8], F32)
-        grouped = sb.tile([P, 2 * N, 4], BF16, align_bytes=64)
-        codes = sb.tile([P, 2 * N], U32, align_bytes=64)
-        xsc = sb.tile([P, 2 * N], U8, align_bytes=64)
-        sig = sb.tile([P, 2, 2 * N], F32, align_bytes=64)
-        res = sb.tile([P, 2, 2 * N], F32, align_bytes=64)
-        raw = [sb.tile([P, 4, hi - lo], F32, name="raw%d" % lo, align_bytes=64) for lo, hi in LOADS]
+        grouped = sb.tile([P, 2 * N, 4], BF16, align_bytes=256)
+        codes = sb.tile([P, 2 * N], U32, align_bytes=256)
+        xsc = sb.tile([P, 2 * N], U8, align_bytes=256)
+        sig = sb.tile([P, 2, 2 * N], F32, align_bytes=256)
+        res = sb.tile([P, 2, 2 * N], F32, align_bytes=256)
+        raw = [sb.tile([P, 4, hi - lo], F32, name="raw%d" % lo, align_bytes=256) for lo, hi in LOADS]
         bank = [[ps.tile([P, NT], F32, name="bank%d_%d" % (c, i)) for i in range(4)] for c in range(2)]
         wsrc = [w_words, u_words]
         ssrc = [w_scales, u_scales]

@@ -17,9 +17,16 @@ ALU = mybir.AluOpType
 
 P = 128
 ROWS = 64
-NT = 512
-LOADS = [[0,512],[512,1024],[1024,1408],[1408,1792],[1792,2048]]
-BANKS = [[0,1],[2,3],[0,1],[2,3],[0,1]]
+QUAD = 32
+PASS = 512
+W = 256
+STEPS = 2 * N // W
+LAST = STEPS - 1
+PAD = PASS - W
+ALIGN = 256
+V_EVEN = 128
+V_MORE = 160
+U_PASS = [1, 1, 3, 3, 4, 6, 6, 7]
 
 
 def tile_rows_gglu_sigmoid_kernel(tc, x, w_words, w_scales, u_words, u_scales, out):
@@ -29,166 +36,126 @@ def tile_rows_gglu_sigmoid_kernel(tc, x, w_words, w_scales, u_words, u_scales, o
         ps = ctx.enter_context(tc.psum_pool(name="ps", bufs=1))
         ctx.enter_context(tc.manual_schedule())
 
-        words = [sb.tile([P, 2, 2 * M], U8, name="words%d" % a, align_bytes=256) for a in range(2)]
-        wsc = [sb.tile([P, 2, M], U8, name="wsc%d" % a, align_bytes=256) for a in range(2)]
+        words = [sb.tile([P, 2, 2 * M], U8, name="words%d" % a, align_bytes=ALIGN) for a in range(2)]
+        wsc = [sb.tile([P, 2, M], U8, name="wsc%d" % a, align_bytes=ALIGN) for a in range(2)]
         warm_in = sb.tile([P, 8], F32)
         warm_out = sb.tile([P, 8], F32)
-        grouped = sb.tile([P, 2 * N, 4], BF16, align_bytes=256)
-        codes = sb.tile([P, 2 * N], U32, align_bytes=256)
-        xsc = sb.tile([P, 2 * N], U8, align_bytes=256)
-        sig = sb.tile([P, 2, 2 * N], F32, align_bytes=256)
-        res = sb.tile([P, 2, 2 * N], F32, align_bytes=256)
-        raw = [sb.tile([P, 4, hi - lo], F32, name="raw%d" % lo, align_bytes=256) for lo, hi in LOADS]
-        bank = [[ps.tile([P, NT], F32, name="bank%d_%d" % (c, i)) for i in range(4)] for c in range(2)]
+        grouped = sb.tile([P, 2 * N, 4], BF16, align_bytes=ALIGN)
+        codes = sb.tile([P, PAD + 2 * N], U32, align_bytes=ALIGN)
+        xsc = sb.tile([P, PAD + 2 * N], U8, align_bytes=ALIGN)
+        sig = sb.tile([P, 2, 2 * N], F32, align_bytes=ALIGN)
+        res = sb.tile([P, 2, 2 * N], F32, align_bytes=ALIGN)
+        raw = [sb.tile([P, 4, W], F32, name="raw%d" % k, align_bytes=ALIGN) for k in range(STEPS)]
+        zbank = [[ps.tile([P, PASS], F32, name="z%d_%d" % (c, i)) for i in range(2)] for c in range(2)]
+        ubank = [[ps.tile([P, PASS], F32, name="u%d_%d" % (c, i)) for i in range(2)] for c in range(2)]
+        u_passes = sorted(set(U_PASS))
         wsrc = [w_words, u_words]
         ssrc = [w_scales, u_scales]
 
-        def load_words(eng, a):
-            eng.dma_start(
+        def load_words(a):
+            nc.sync.dma_start(
                 out=words[a][:].bitcast(I32),
                 in_=wsrc[a].rearrange("(s c) p b -> (c p) s b", c=2).bitcast(I32),
             )
 
-        def load_scales(eng, a):
+        def load_scales(a):
             for q in range(4):
-                eng.dma_start(
-                    out=wsc[a][32 * q : 32 * q + 4, :, :].bitcast(I32),
+                nc.sync.dma_start(
+                    out=wsc[a][QUAD * q : QUAD * q + 4, :, :].bitcast(I32),
                     in_=ssrc[a].rearrange("(s c) (h r) m -> (c h) r s m", c=2, r=4)[q].bitcast(I32),
                 )
 
-        def load_x(k, eng=nc.sync):
-            lo, hi = LOADS[k]
-            s = lo // N
-            src = x[2 * s : 2 * s + 2].rearrange("c (p j) n -> (c p) j n", j=4)
-            eng.dma_start(out=raw[k][:], in_=src[:, :, lo - s * N : hi - s * N])
+        def load_x(k):
+            s, lo = divmod(k * W, N)
+            src = x[2 * s : 2 * s + 2].rearrange("c (p t) n -> (c p) t n", t=4)
+            nc.sync.dma_start(out=raw[k][:], in_=src[:, :, lo : lo + W])
 
-        def views(lo, hi):
-            k = [i for i in range(len(LOADS)) if LOADS[i][0] <= lo and hi <= LOADS[i][1]][0]
-            o = LOADS[k][0]
-            dst = grouped[:, lo:hi, :].rearrange("p (c i) t -> p c t i", i=4)
-            src = raw[k][:, :, lo - o : hi - o].rearrange("p t (c i) -> p c t i", i=4)
-            return dst, src
+        def interleave(k):
+            v = V_EVEN if 3 <= k < LAST else V_MORE
+            dst = grouped[:, k * W : (k + 1) * W, :].rearrange("p (c i) t -> p c t i", i=4)
+            src = raw[k][:].rearrange("p t (c i) -> p c t i", i=4)
+            nc.vector.tensor_copy(out=dst[:, : v // 4], in_=src[:, : v // 4])
+            nc.scalar.copy(out=dst[:, v // 4 :], in_=src[:, v // 4 :])
 
-        def copy_v(lo, hi):
-            dst, src = views(lo, hi)
-            nc.vector.tensor_copy(out=dst, in_=src)
-
-        def copy_s(lo, hi):
-            dst, src = views(lo, hi)
-            nc.scalar.copy(out=dst, in_=src)
-
-        def copy_g(lo, hi):
-            dst, src = views(lo, hi)
-            nc.gpsimd.tensor_scalar(out=dst, in0=src, scalar1=1.0, scalar2=0.0, op0=ALU.mult, op1=ALU.add)
-
-        def quant(lo, hi):
+        def quantise(k):
+            cols = slice(PAD + k * W, PAD + (k + 1) * W)
             nc.vector.quantize_mx(
-                out=codes[:, lo:hi].bitcast(FP8X4),
-                scales=xsc[:, lo:hi],
-                in_=grouped[:, lo:hi, :].rearrange("p c t -> p (c t)"),
+                out=codes[:, cols].bitcast(FP8X4),
+                scales=xsc[:, cols],
+                in_=grouped[:, k * W : (k + 1) * W, :].rearrange("p c t -> p (c t)"),
             )
 
-        def product(a, k):
-            lo, hi = LOADS[k]
-            s = lo // N
+        def passes(a, k, banks):
+            s = k * W // N
+            cols = slice(k * W, k * W + PASS)
             for c in range(2):
                 r = slice(ROWS * c, ROWS * (c + 1))
                 nc.tensor.matmul_mx(
-                    out=bank[c][BANKS[k][a]][:],
+                    out=banks[c][:],
                     lhsT=words[a][r, s, :].bitcast(FP4X4),
                     lhsT_scale=wsc[a][r, s, :],
-                    rhs=codes[r, hi - NT : hi].bitcast(FP8X4),
-                    rhs_scale=xsc[r, hi - NT : hi],
+                    rhs=codes[r, cols].bitcast(FP8X4),
+                    rhs_scale=xsc[r, cols],
                     start=True,
                     stop=True,
                 )
 
-        def mm(k):
-            product(0, k)
-            product(1, k)
+        def w_passes(k):
+            passes(0, k, [zbank[c][k % 2] for c in range(2)])
 
-        def sg(k, c):
-            lo, hi = LOADS[k]
-            nc.scalar.activation(out=sig[:, c, lo:hi], in_=bank[c][BANKS[k][0]][:, NT - (hi - lo) :], func=ACT.Sigmoid)
+        def u_pass(k):
+            if k in u_passes:
+                passes(1, k, [ubank[c][u_passes.index(k) % 2] for c in range(2)])
 
-        def gt(k, c):
-            lo, hi = LOADS[k]
-            nc.vector.tensor_tensor(
-                out=res[:, c, lo:hi], in0=bank[c][BANKS[k][1]][:, NT - (hi - lo) :], in1=sig[:, c, lo:hi], op=ALU.mult
-            )
+        def sigmoids(k):
+            for c in range(2):
+                nc.scalar.activation(out=sig[:, c, k * W : (k + 1) * W], in_=zbank[c][k % 2][:, PAD:], func=ACT.Sigmoid)
 
-        def st(k, c):
-            store(c, LOADS[k][0], LOADS[k][1])
-
-        def st2(k):
-            lo, hi = LOADS[k]
+        def store(lo, hi, c0, c1):
             s = lo // N
-            nc.sync.dma_start(
-                out=out[2 * s : 2 * s + 2, :, lo - s * N : hi - s * N].rearrange("c m n -> m c n"), in_=res[:, :, lo:hi]
-            )
+            dst = out[2 * s + c0 : 2 * s + c1, :, lo - s * N : hi - s * N].rearrange("c m n -> m c n")
+            nc.sync.dma_start(out=dst, in_=res[:, c0:c1, lo:hi])
 
-        def cp(k, v):
-            lo, hi = LOADS[k]
-            if v > 0:
-                copy_v(lo, lo + v)
-            if lo + v < hi:
-                copy_s(lo + v, hi)
-
-        def qq(k):
-            lo, hi = LOADS[k]
-            for a in range(lo, hi, 256):
-                quant(a, min(a + 256, hi))
-
-        def store(c, lo, hi, eng=nc.sync):
-            s = lo // N
-            eng.dma_start(out=out[2 * s + c, :, lo - s * N : hi - s * N], in_=res[:, c, lo:hi])
+        def gate(k, c):
+            lo, hi = k * W, (k + 1) * W
+            first = PAD - (U_PASS[k] - k) * W
+            bank = ubank[c][u_passes.index(U_PASS[k]) % 2]
+            nc.vector.tensor_tensor(out=res[:, c, lo:hi], in0=bank[:, first : first + W], in1=sig[:, c, lo:hi], op=ALU.mult)
+            if lo >= N:
+                store(lo, hi, c, c + 1)
+            elif c == 1 and k >= 1:
+                store(lo if k > 1 else 0, hi, 0, 2)
 
         for a in range(2):
             nc.vector.memset(wsc[a][:].rearrange("p s m -> p (s m)").bitcast(I32), 0)
         nc.vector.memset(warm_in[:], 0.0)
         nc.scalar.activation(out=warm_out[:], in_=warm_in[:], func=ACT.Sigmoid)
-        def words_pair(a, s):
-            nc.sync.dma_start(
-                out=words[a][:, s, :].bitcast(I32),
-                in_=wsrc[a][2 * s : 2 * s + 2].rearrange("c p b -> (c p) b").bitcast(I32),
-            )
+        nc.vector.memset(codes[:, :PAD], 0)
+        nc.vector.memset(xsc[:, :PAD].bitcast(U32), 0)
 
         load_x(0)
-        load_scales(nc.sync, 0)
+        load_scales(0)
+        load_words(0)
         load_x(1)
-        words_pair(0, 0)
-        words_pair(1, 0)
-        load_scales(nc.sync, 1)
         load_x(2)
-        words_pair(0, 1)
-        words_pair(1, 1)
-        load_x(3)
-        load_x(4)
-        SHARE = [320,384,192,192,128]
-        last = len(LOADS) - 1
+        load_words(1)
+        load_scales(1)
+        for k in range(3, STEPS):
+            load_x(k)
 
-        def out_of(k, c):
-            gt(k, c)
-            st(k, c)
-
-        for k in range(last):
-            cp(k, SHARE[k])
-            if k >= 1:
-                sg(k - 1, 0)
-            if k >= 2:
-                out_of(k - 2, 1)
-            qq(k)
-            mm(k)
-            if 1 <= k < last - 1:
-                sg(k - 1, 1)
-                out_of(k - 1, 0)
-        cp(last, SHARE[last])
-        sg(last - 2, 1)
-        out_of(last - 2, 0)
-        qq(last)
-        out_of(last - 2, 1)
-        mm(last)
-        for k in (last - 1, last):
-            for c in range(2):
-                sg(k, c)
-                out_of(k, c)
+        for k in range(STEPS + 3):
+            if k < STEPS:
+                interleave(k)
+            if 2 <= k < STEPS + 2:
+                sigmoids(k - 2)
+            if k >= 3:
+                gate(k - 3, 0)
+            if k == LAST:
+                quantise(k)
+                w_passes(k)
+            if k >= 3:
+                gate(k - 3, 1)
+            if k < LAST:
+                quantise(k)
+                w_passes(k)
+            u_pass(k)

@@ -72,10 +72,10 @@ def tile_rows_gglu_sigmoid_kernel(tc, x, w_words, w_scales, u_words, u_scales, o
 
         def interleave(k):
             v = V_EVEN if 3 <= k < LAST else V_MORE
-            dst = grouped[:, k * W : (k + 1) * W, :].rearrange("p (c i) t -> p c t i", i=4)
-            src = raw[k][:].rearrange("p t (c i) -> p c t i", i=4)
-            nc.vector.tensor_copy(out=dst[:, : v // 4], in_=src[:, : v // 4])
-            nc.scalar.copy(out=dst[:, v // 4 :], in_=src[:, v // 4 :])
+            dst = grouped[:, k * W : (k + 1) * W, :].rearrange("p (c i) t -> p c t i", i=2)
+            src = raw[k][:].rearrange("p t (c i) -> p c t i", i=2)
+            nc.vector.tensor_copy(out=dst[:, : v // 2], in_=src[:, : v // 2])
+            nc.scalar.copy(out=dst[:, v // 2 :], in_=src[:, v // 2 :])
 
         def quantise(k):
             cols = slice(PAD + k * W, PAD + (k + 1) * W)

@@ -85,27 +85,27 @@ def tile_rows_gglu_sigmoid_kernel(tc, x, w_words, w_scales, u_words, u_scales, o
                 in_=grouped[:, k * W : (k + 1) * W, :].rearrange("p c t -> p (c t)"),
             )
 
-        def passes(a, k, banks):
+        def mx_pass(a, k, c, bank):
             s = k * W // N
             cols = slice(k * W, k * W + PASS)
-            for c in range(2):
-                r = slice(ROWS * c, ROWS * (c + 1))
-                nc.tensor.matmul_mx(
-                    out=banks[c][:],
-                    lhsT=words[a][r, s, :].bitcast(FP4X4),
-                    lhsT_scale=wsc[a][r, s, :],
-                    rhs=codes[r, cols].bitcast(FP8X4),
-                    rhs_scale=xsc[r, cols],
-                    start=True,
-                    stop=True,
-                )
+            r = slice(ROWS * c, ROWS * (c + 1))
+            nc.tensor.matmul_mx(
+                out=bank[:],
+                lhsT=words[a][r, s, :].bitcast(FP4X4),
+                lhsT_scale=wsc[a][r, s, :],
+                rhs=codes[r, cols].bitcast(FP8X4),
+                rhs_scale=xsc[r, cols],
+                start=True,
+                stop=True,
+            )
 
         def w_passes(k):
-            passes(0, k, [zbank[c][k % 2] for c in range(2)])
+            for c in range(2):
+                mx_pass(0, k, c, zbank[c][k % 2])
 
-        def u_pass(k):
+        def u_pass(k, c):
             if k in u_passes:
-                passes(1, k, [ubank[c][u_passes.index(k) % 2] for c in range(2)])
+                mx_pass(1, k, c, ubank[c][u_passes.index(k) % 2])
 
         def sigmoids(k):
             for c in range(2):
@@ -143,19 +143,25 @@ def tile_rows_gglu_sigmoid_kernel(tc, x, w_words, w_scales, u_words, u_scales, o
         for k in range(3, STEPS):
             load_x(k)
 
-        for k in range(STEPS + 3):
-            if k < STEPS:
-                interleave(k)
-            if 2 <= k < STEPS + 2:
+        results = [(k, c) for k in range(STEPS) for c in range(2)]
+        for k in range(STEPS):
+            interleave(k)
+            if k >= 2:
                 sigmoids(k - 2)
             if k >= 3:
-                gate(k - 3, 0)
+                for n in range(2 if k < LAST - 1 else 1):
+                    gate(*results.pop(0))
             if k == LAST:
-                quantise(k)
-                w_passes(k)
-            if k >= 3:
-                gate(k - 3, 1)
+                u_pass(k - 1, 1)
+            quantise(k)
+            w_passes(k)
             if k < LAST:
-                quantise(k)
-                w_passes(k)
-            u_pass(k)
+                u_pass(k, 0)
+            if k < LAST - 1:
+                u_pass(k, 1)
+        sigmoids(LAST - 1)
+        sigmoids(LAST)
+        for k, c in results:
+            gate(k, c)
+            if k == STEPS // 2:
+                u_pass(LAST, c)

@@ -19,14 +19,16 @@ P = 128
 ROWS = 64
 QUAD = 32
 PASS = 512
-W = 256
-STEPS = 2 * N // W
-LAST = STEPS - 1
-PAD = PASS - W
 ALIGN = 256
-V_EVEN = 128
-V_MORE = 160
-U_PASS = [1, 1, 3, 3, 4, 6, 6, 7]
+WIDTHS = [256, 256, 256, 256, 256, 256, 256, 256]
+STEPS = len(WIDTHS)
+LAST = STEPS - 1
+EDGE = [sum(WIDTHS[:k]) for k in range(STEPS + 1)]
+PAD = PASS - WIDTHS[0]
+VSHARE = [160, 160, 160, 128, 128, 128, 128, 160]
+SERVED_BY = [[0, 2, 2, 3, 4, 6, 6, 7], [1, 1, 3, 3, 4, 6, 6, 7]]
+SIGS = [max(k, 2 * k - 3) for k in range(STEPS)]
+GATES = [max(0, 2 * k - 5) for k in range(LAST)] + [2 * LAST - 6]
 
 
 def tile_rows_gglu_sigmoid_kernel(tc, x, w_words, w_scales, u_words, u_scales, out):
@@ -40,15 +42,14 @@ def tile_rows_gglu_sigmoid_kernel(tc, x, w_words, w_scales, u_words, u_scales, o
         wsc = [sb.tile([P, 2, M], U8, name="wsc%d" % a, align_bytes=ALIGN) for a in range(2)]
         warm_in = sb.tile([P, 8], F32)
         warm_out = sb.tile([P, 8], F32)
-        grouped = sb.tile([P, 2 * N, 4], BF16, align_bytes=ALIGN)
+        grouped = [sb.tile([P, max(WIDTHS), 4], BF16, name="grouped%d" % i, align_bytes=ALIGN) for i in range(STEPS)]
         codes = sb.tile([P, PAD + 2 * N], U32, align_bytes=ALIGN)
         xsc = sb.tile([P, PAD + 2 * N], U8, align_bytes=ALIGN)
         sig = sb.tile([P, 2, 2 * N], F32, align_bytes=ALIGN)
         res = sb.tile([P, 2, 2 * N], F32, align_bytes=ALIGN)
-        raw = [sb.tile([P, 4, W], F32, name="raw%d" % k, align_bytes=ALIGN) for k in range(STEPS)]
-        zbank = [[ps.tile([P, PASS], F32, name="z%d_%d" % (c, i)) for i in range(2)] for c in range(2)]
-        ubank = [[ps.tile([P, PASS], F32, name="u%d_%d" % (c, i)) for i in range(2)] for c in range(2)]
-        u_passes = sorted(set(U_PASS))
+        raw = [sb.tile([P, 4, max(WIDTHS)], F32, name="raw%d" % k, align_bytes=ALIGN) for k in range(STEPS)]
+        banks = [[[ps.tile([P, PASS], F32, name="bank%d_%d_%d" % (a, c, i)) for i in range(2)] for c in range(2)] for a in range(2)]
+        ends = [sorted(set(SERVED_BY[a])) for a in range(2)]
         wsrc = [w_words, u_words]
         ssrc = [w_scales, u_scales]
 
@@ -58,39 +59,45 @@ def tile_rows_gglu_sigmoid_kernel(tc, x, w_words, w_scales, u_words, u_scales, o
                 in_=wsrc[a].rearrange("(s c) p b -> (c p) s b", c=2).bitcast(I32),
             )
 
-        def load_scales(a):
-            for q in range(4):
+        def load_scales(a, c):
+            for q in (2 * c, 2 * c + 1):
                 nc.sync.dma_start(
                     out=wsc[a][QUAD * q : QUAD * q + 4, :, :].bitcast(I32),
                     in_=ssrc[a].rearrange("(s c) (h r) m -> (c h) r s m", c=2, r=4)[q].bitcast(I32),
                 )
 
         def load_x(k):
-            s, lo = divmod(k * W, N)
+            s, lo = divmod(EDGE[k], N)
             src = x[2 * s : 2 * s + 2].rearrange("c (p t) n -> (c p) t n", t=4)
-            nc.sync.dma_start(out=raw[k][:], in_=src[:, :, lo : lo + W])
+            nc.sync.dma_start(out=raw[k][:, :, : WIDTHS[k]], in_=src[:, :, lo : lo + WIDTHS[k]])
 
-        def interleave(k):
-            v = V_EVEN if 3 <= k < LAST else V_MORE
-            dst = grouped[:, k * W : (k + 1) * W, :].rearrange("p (c i) t -> p c t i", i=2)
-            src = raw[k][:].rearrange("p t (c i) -> p c t i", i=2)
-            nc.vector.tensor_copy(out=dst[:, : v // 2], in_=src[:, : v // 2])
-            nc.scalar.copy(out=dst[:, v // 2 :], in_=src[:, v // 2 :])
+        def views(k, lo, hi):
+            dst = grouped[k % len(grouped)][:, lo:hi, :].rearrange("p (c i) t -> p c t i", i=2)
+            src = raw[k][:, :, lo:hi].rearrange("p t (c i) -> p c t i", i=2)
+            return dst, src
+
+        def copy_v(k, lo, hi):
+            dst, src = views(k, lo, hi)
+            nc.vector.tensor_copy(out=dst, in_=src)
+
+        def copy_s(k, lo, hi):
+            dst, src = views(k, lo, hi)
+            nc.scalar.copy(out=dst, in_=src)
 
         def quantise(k):
-            cols = slice(PAD + k * W, PAD + (k + 1) * W)
+            cols = slice(PAD + EDGE[k], PAD + EDGE[k + 1])
             nc.vector.quantize_mx(
                 out=codes[:, cols].bitcast(FP8X4),
                 scales=xsc[:, cols],
-                in_=grouped[:, k * W : (k + 1) * W, :].rearrange("p c t -> p (c t)"),
+                in_=grouped[k % len(grouped)][:, : WIDTHS[k], :].rearrange("p c t -> p (c t)"),
             )
 
-        def mx_pass(a, k, c, bank):
-            s = k * W // N
-            cols = slice(k * W, k * W + PASS)
+        def mx_pass(a, k, c):
+            s = EDGE[k] // N
+            cols = slice(PAD + EDGE[k + 1] - PASS, PAD + EDGE[k + 1])
             r = slice(ROWS * c, ROWS * (c + 1))
             nc.tensor.matmul_mx(
-                out=bank[:],
+                out=banks[a][c][ends[a].index(k) % 2][:],
                 lhsT=words[a][r, s, :].bitcast(FP4X4),
                 lhsT_scale=wsc[a][r, s, :],
                 rhs=codes[r, cols].bitcast(FP8X4),
@@ -99,69 +106,86 @@ def tile_rows_gglu_sigmoid_kernel(tc, x, w_words, w_scales, u_words, u_scales, o
                 stop=True,
             )
 
-        def w_passes(k):
-            for c in range(2):
-                mx_pass(0, k, c, zbank[c][k % 2])
+        def held(a, k, c):
+            end = SERVED_BY[a][k]
+            first = PASS - (EDGE[end + 1] - EDGE[k])
+            return banks[a][c][ends[a].index(end) % 2][:, first : first + WIDTHS[k]]
 
-        def u_pass(k, c):
-            if k in u_passes:
-                mx_pass(1, k, c, ubank[c][u_passes.index(k) % 2])
-
-        def sigmoids(k):
-            for c in range(2):
-                nc.scalar.activation(out=sig[:, c, k * W : (k + 1) * W], in_=zbank[c][k % 2][:, PAD:], func=ACT.Sigmoid)
-
-        def store(lo, hi, c0, c1):
-            s = lo // N
-            dst = out[2 * s + c0 : 2 * s + c1, :, lo - s * N : hi - s * N].rearrange("c m n -> m c n")
-            nc.sync.dma_start(out=dst, in_=res[:, c0:c1, lo:hi])
+        def sigmoid(k, c):
+            cols = slice(EDGE[k], EDGE[k + 1])
+            nc.scalar.activation(out=sig[:, c, cols], in_=held(0, k, c), func=ACT.Sigmoid)
 
         def gate(k, c):
-            lo, hi = k * W, (k + 1) * W
-            first = PAD - (U_PASS[k] - k) * W
-            bank = ubank[c][u_passes.index(U_PASS[k]) % 2]
-            nc.vector.tensor_tensor(out=res[:, c, lo:hi], in0=bank[:, first : first + W], in1=sig[:, c, lo:hi], op=ALU.mult)
-            if lo >= N:
-                store(lo, hi, c, c + 1)
-            elif c == 1 and k >= 1:
-                store(lo if k > 1 else 0, hi, 0, 2)
+            cols = slice(EDGE[k], EDGE[k + 1])
+            nc.vector.tensor_tensor(out=res[:, c, cols], in0=held(1, k, c), in1=sig[:, c, cols], op=ALU.mult)
 
-        for a in range(2):
-            nc.vector.memset(wsc[a][:].rearrange("p s m -> p (s m)").bitcast(I32), 0)
+        def store(k0, k1, c0, c1):
+            s, lo = divmod(EDGE[k0], N)
+            dst = out[2 * s + c0 : 2 * s + c1, :, lo : lo + EDGE[k1 + 1] - EDGE[k0]].rearrange("c m n -> m c n")
+            nc.sync.dma_start(out=dst, in_=res[:, c0:c1, EDGE[k0] : EDGE[k1 + 1]])
+
         nc.vector.memset(warm_in[:], 0.0)
         nc.scalar.activation(out=warm_out[:], in_=warm_in[:], func=ACT.Sigmoid)
+        for a in range(2):
+            nc.vector.memset(wsc[a][:].rearrange("p s m -> p (s m)").bitcast(I32), 0)
         nc.vector.memset(codes[:, :PAD], 0)
         nc.vector.memset(xsc[:, :PAD].bitcast(U32), 0)
 
         load_x(0)
-        load_scales(0)
+        load_scales(0, 0)
+        load_scales(0, 1)
         load_words(0)
         load_x(1)
         load_x(2)
         load_words(1)
-        load_scales(1)
+        load_scales(1, 0)
+        load_scales(1, 1)
         for k in range(3, STEPS):
             load_x(k)
 
-        results = [(k, c) for k in range(STEPS) for c in range(2)]
-        for k in range(STEPS):
-            interleave(k)
-            if k >= 2:
-                sigmoids(k - 2)
-            if k >= 3:
-                for n in range(2 if k < LAST - 1 else 1):
-                    gate(*results.pop(0))
-            if k == LAST:
-                u_pass(k - 1, 1)
-            quantise(k)
-            w_passes(k)
-            if k < LAST:
-                u_pass(k, 0)
-            if k < LAST - 1:
-                u_pass(k, 1)
-        sigmoids(LAST - 1)
-        sigmoids(LAST)
-        for k, c in results:
+        quantised, passed = [], []
+        read = [[], []]
+
+        def bank_free(a, k, c):
+            i = ends[a].index(k)
+            return i < 2 or all((j, c) in read[a] for j in range(STEPS) if SERVED_BY[a][j] == ends[a][i - 2])
+
+        def issue_passes():
+            for k in quantised:
+                for a in range(2):
+                    for c in range(2):
+                        if k in ends[a] and (a, k, c) not in passed and bank_free(a, k, c):
+                            mx_pass(a, k, c)
+                            passed.append((a, k, c))
+
+        def next_sigmoid():
+            k, c = divmod(len(read[0]), 2)
+            sigmoid(k, c)
+            read[0].append((k, c))
+            issue_passes()
+
+        def next_gate():
+            k, c = divmod(len(read[1]), 2)
             gate(k, c)
-            if k == STEPS // 2:
-                u_pass(LAST, c)
+            read[1].append((k, c))
+            issue_passes()
+            if k >= 4:
+                store(k, k, c, c + 1)
+            elif c == 1 and k >= 1:
+                store(k if k > 1 else 0, k, 0, 2)
+
+        for k in range(STEPS):
+            v = VSHARE[k]
+            copy_v(k, 0, v)
+            copy_s(k, v, WIDTHS[k])
+            while len(read[0]) < SIGS[k]:
+                next_sigmoid()
+            while len(read[1]) < GATES[k]:
+                next_gate()
+            quantise(k)
+            quantised.append(k)
+            issue_passes()
+        while len(read[1]) < 2 * STEPS:
+            if len(read[0]) < 2 * STEPS:
+                next_sigmoid()
+            next_gate()

from contextlib import ExitStack

import concourse.mybir as mybir

G, D, M, N = 4, 256, 128, 1024
FLOPS = 2 * 2 * G * D * M * N

F32 = mybir.dt.float32
BF16 = mybir.dt.bfloat16
I32 = mybir.dt.int32
U32 = mybir.dt.uint32
U8 = mybir.dt.uint8
FP8X4 = mybir.dt.float8_e4m3fn_x4
FP4X4 = mybir.dt.float4_e2m1fn_x4
ACT = mybir.ActivationFunctionType
ALU = mybir.AluOpType

P = 128
ROWS = 64
QUAD = 32
PASS = 512
ALIGN = 256
WIDTHS = [256, 256, 256, 256, 256, 256, 256, 256]
STEPS = len(WIDTHS)
LAST = STEPS - 1
EDGE = [sum(WIDTHS[:k]) for k in range(STEPS + 1)]
PAD = PASS - WIDTHS[0]
VSHARE = [160, 160, 160, 128, 128, 128, 128, 160]
SERVED_BY = [[0, 2, 2, 3, 4, 6, 6, 7], [1, 1, 3, 3, 4, 6, 6, 7]]
SIGS = [max(k, 2 * k - 3) for k in range(STEPS)]
GATES = [max(0, 2 * k - 5) for k in range(LAST)] + [2 * LAST - 6]


def tile_rows_gglu_sigmoid_kernel(tc, x, w_words, w_scales, u_words, u_scales, out):
    nc = tc.nc
    with ExitStack() as ctx:
        sb = ctx.enter_context(tc.tile_pool(name="sb", bufs=1))
        ps = ctx.enter_context(tc.psum_pool(name="ps", bufs=1))
        ctx.enter_context(tc.manual_schedule())

        words = [sb.tile([P, 2, 2 * M], U8, name="words%d" % a, align_bytes=ALIGN) for a in range(2)]
        wsc = [sb.tile([P, 2, M], U8, name="wsc%d" % a, align_bytes=ALIGN) for a in range(2)]
        warm_in = sb.tile([P, 8], F32)
        warm_out = sb.tile([P, 8], F32)
        grouped = [sb.tile([P, max(WIDTHS), 4], BF16, name="grouped%d" % i, align_bytes=ALIGN) for i in range(STEPS)]
        codes = sb.tile([P, PAD + 2 * N], U32, align_bytes=ALIGN)
        xsc = sb.tile([P, PAD + 2 * N], U8, align_bytes=ALIGN)
        sig = sb.tile([P, 2, 2 * N], F32, align_bytes=ALIGN)
        res = sb.tile([P, 2, 2 * N], F32, align_bytes=ALIGN)
        raw = [sb.tile([P, 4, max(WIDTHS)], F32, name="raw%d" % k, align_bytes=ALIGN) for k in range(STEPS)]
        banks = [[[ps.tile([P, PASS], F32, name="bank%d_%d_%d" % (a, c, i)) for i in range(2)] for c in range(2)] for a in range(2)]
        ends = [sorted(set(SERVED_BY[a])) for a in range(2)]
        wsrc = [w_words, u_words]
        ssrc = [w_scales, u_scales]

        def load_words(a):
            nc.sync.dma_start(
                out=words[a][:].bitcast(I32),
                in_=wsrc[a].rearrange("(s c) p b -> (c p) s b", c=2).bitcast(I32),
            )

        def load_scales(a, c):
            for q in (2 * c, 2 * c + 1):
                nc.sync.dma_start(
                    out=wsc[a][QUAD * q : QUAD * q + 4, :, :].bitcast(I32),
                    in_=ssrc[a].rearrange("(s c) (h r) m -> (c h) r s m", c=2, r=4)[q].bitcast(I32),
                )

        def load_x(k):
            s, lo = divmod(EDGE[k], N)
            src = x[2 * s : 2 * s + 2].rearrange("c (p t) n -> (c p) t n", t=4)
            nc.sync.dma_start(out=raw[k][:, :, : WIDTHS[k]], in_=src[:, :, lo : lo + WIDTHS[k]])

        def views(k, lo, hi):
            dst = grouped[k % len(grouped)][:, lo:hi, :].rearrange("p (c i) t -> p c t i", i=2)
            src = raw[k][:, :, lo:hi].rearrange("p t (c i) -> p c t i", i=2)
            return dst, src

        def copy_v(k, lo, hi):
            dst, src = views(k, lo, hi)
            nc.vector.tensor_copy(out=dst, in_=src)

        def copy_s(k, lo, hi):
            dst, src = views(k, lo, hi)
            nc.scalar.copy(out=dst, in_=src)

        def quantise(k):
            cols = slice(PAD + EDGE[k], PAD + EDGE[k + 1])
            nc.vector.quantize_mx(
                out=codes[:, cols].bitcast(FP8X4),
                scales=xsc[:, cols],
                in_=grouped[k % len(grouped)][:, : WIDTHS[k], :].rearrange("p c t -> p (c t)"),
            )

        def mx_pass(a, k, c):
            s = EDGE[k] // N
            cols = slice(PAD + EDGE[k + 1] - PASS, PAD + EDGE[k + 1])
            r = slice(ROWS * c, ROWS * (c + 1))
            nc.tensor.matmul_mx(
                out=banks[a][c][ends[a].index(k) % 2][:],
                lhsT=words[a][r, s, :].bitcast(FP4X4),
                lhsT_scale=wsc[a][r, s, :],
                rhs=codes[r, cols].bitcast(FP8X4),
                rhs_scale=xsc[r, cols],
                start=True,
                stop=True,
            )

        def held(a, k, c):
            end = SERVED_BY[a][k]
            first = PASS - (EDGE[end + 1] - EDGE[k])
            return banks[a][c][ends[a].index(end) % 2][:, first : first + WIDTHS[k]]

        def sigmoid(k, c):
            cols = slice(EDGE[k], EDGE[k + 1])
            nc.scalar.activation(out=sig[:, c, cols], in_=held(0, k, c), func=ACT.Sigmoid)

        def gate(k, c):
            cols = slice(EDGE[k], EDGE[k + 1])
            nc.vector.tensor_tensor(out=res[:, c, cols], in0=held(1, k, c), in1=sig[:, c, cols], op=ALU.mult)

        def store(k0, k1, c0, c1):
            s, lo = divmod(EDGE[k0], N)
            dst = out[2 * s + c0 : 2 * s + c1, :, lo : lo + EDGE[k1 + 1] - EDGE[k0]].rearrange("c m n -> m c n")
            nc.sync.dma_start(out=dst, in_=res[:, c0:c1, EDGE[k0] : EDGE[k1 + 1]])

        nc.vector.memset(warm_in[:], 0.0)
        nc.scalar.activation(out=warm_out[:], in_=warm_in[:], func=ACT.Sigmoid)
        for a in range(2):
            nc.vector.memset(wsc[a][:].rearrange("p s m -> p (s m)").bitcast(I32), 0)
        nc.vector.memset(codes[:, :PAD], 0)
        nc.vector.memset(xsc[:, :PAD].bitcast(U32), 0)

        load_x(0)
        load_scales(0, 0)
        load_scales(0, 1)
        load_words(0)
        load_x(1)
        load_x(2)
        load_words(1)
        load_scales(1, 0)
        load_scales(1, 1)
        for k in range(3, STEPS):
            load_x(k)

        quantised, passed = [], []
        read = [[], []]

        def bank_free(a, k, c):
            i = ends[a].index(k)
            return i < 2 or all((j, c) in read[a] for j in range(STEPS) if SERVED_BY[a][j] == ends[a][i - 2])

        def issue_passes():
            for k in quantised:
                for a in range(2):
                    for c in range(2):
                        if k in ends[a] and (a, k, c) not in passed and bank_free(a, k, c):
                            mx_pass(a, k, c)
                            passed.append((a, k, c))

        def next_sigmoid():
            k, c = divmod(len(read[0]), 2)
            sigmoid(k, c)
            read[0].append((k, c))
            issue_passes()

        def next_gate():
            k, c = divmod(len(read[1]), 2)
            gate(k, c)
            read[1].append((k, c))
            issue_passes()
            if k >= 4:
                store(k, k, c, c + 1)
            elif c == 1 and k >= 1:
                store(k if k > 1 else 0, k, 0, 2)

        for k in range(STEPS):
            v = VSHARE[k]
            copy_v(k, 0, v)
            copy_s(k, v, WIDTHS[k])
            while len(read[0]) < SIGS[k]:
                next_sigmoid()
            while len(read[1]) < GATES[k]:
                next_gate()
            quantise(k)
            quantised.append(k)
            issue_passes()
        while len(read[1]) < 2 * STEPS:
            if len(read[0]) < 2 * STEPS:
                next_sigmoid()
            next_gate()
